import numpy as np
import ml_dtypes


def mxq(x, axis, fmt="e4m3"):
    dtype, down = {"e4m3": (ml_dtypes.float8_e4m3fn, 7), "e5m2": (ml_dtypes.float8_e5m2, 14)}[fmt]
    v = np.moveaxis(np.asarray(x, np.float32).astype(ml_dtypes.bfloat16).astype(np.float64), axis, -1)
    blocks = v.reshape(v.shape[:-1] + (-1, 32))
    amax = np.abs(blocks).max(-1, keepdims=True)
    byte = np.maximum(np.where(amax > 0, np.frexp(amax)[1] - 1 + 127, 0) - down, 1)
    scale = np.exp2(byte - 127.0)
    codes = (blocks / scale).astype(np.float32).astype(dtype).astype(np.float64)
    return np.moveaxis((codes * scale).reshape(v.shape), -1, axis)


WIDE = False


def mx_kscale(k):
    if not WIDE:
        return np.ones(k)
    levels = np.array([10, -10, 5, -5, 0])
    if k % 512:
        return np.exp2(np.random.permutation(np.resize(levels, k // 32))).repeat(32)
    a = np.empty((k // 512, 16))
    for p in range(k // 512):
        a[p, :8] = np.random.permutation(np.resize(levels, 8))
        for g in range(8):
            far = levels[np.abs(levels - a[p, g]) >= 10]
            a[p, g + 8] = far[np.random.randint(len(far))]
    return np.exp2(a.ravel()).repeat(32)


def f64(x):
    return np.asarray(x).astype(np.float64)


def striped(idx):
    return np.tile(idx.reshape(-1, 16).T, (8, 1)).astype(np.uint16)


def unstriped(offs):
    return offs[:16].T.reshape(-1).astype(np.int64)


def pack_weight(w):
    k, n = w.shape
    w = f64(np.asarray(w, np.float32).astype(ml_dtypes.bfloat16)).reshape(k // 32, 32, n)
    amax = np.abs(w).max(1)
    byte = np.clip(np.where(amax > 0, np.frexp(amax)[1] - 1 + 127 - 7, 1), 1, 254)
    scaled = (w * np.exp2(127.0 - byte)[:, None, :]).reshape(k, n).astype(np.float32)
    words = np.ascontiguousarray(scaled.reshape(k // 512, 128, 4, n).transpose(0, 1, 3, 2)).astype(ml_dtypes.float8_e4m3fn).view(np.uint8)
    return words, np.ascontiguousarray(byte.astype(np.uint8).reshape(k // 512, 16, n))


def unpack_weight(words, scales):
    g, p, n, _ = words.shape
    vals = np.ascontiguousarray(words).view(ml_dtypes.float8_e4m3fn).astype(np.float64) * np.repeat(np.exp2(scales.astype(np.float64) - 127.0), 8, axis=1)[..., None]
    return vals.transpose(0, 1, 3, 2).reshape(g * 512, n)


K, T, D, S, V, N = 512, 512, 4, 1024, 256, 512


def setup_inputs():
    n = np.random.standard_normal
    s = mx_kscale(K)[:, None]
    words, scales = pack_weight(n((K, N)) / np.sqrt(K) / s)
    return {
        "xT": (n((K, T)) * s).astype(np.float32),
        "w_words": words,
        "w_scales": scales,
        "offs": striped(np.concatenate([np.random.permutation(T)[:V] for _ in range(D)])),
    }


def reference(xT, w_words, w_scales, offs):
    w = unpack_weight(w_words, w_scales)
    idx = unstriped(offs)
    x = np.empty((K, V))
    for l in range(D):
        r = l // 4 * (4 * K // D) + l % 4 + 4 * np.arange(K // D)
        x[r] = f64(xT)[r][:, idx[l * V:(l + 1) * V]]
    xq = mxq(x, 0, "e4m3")
    return w.T @ xq

@@ -1,0 +1,94 @@
+from contextlib import ExitStack
+
+import concourse.mybir as mybir
+
+K, T, D, V, N = 512, 512, 4, 256, 512
+FLOPS = 2 * K * N * V
+
+F32 = mybir.dt.float32
+BF16 = mybir.dt.bfloat16
+I32 = mybir.dt.int32
+U32 = mybir.dt.uint32
+U16 = mybir.dt.uint16
+U8 = mybir.dt.uint8
+FP8X4 = mybir.dt.float8_e4m3fn_x4
+
+P = 128
+HALF = V // 2
+COLS = 16
+
+
+def tile_picked_grid_lin_none_sub_l_kernel(tc, xT, w_words, w_scales, offs, out):
+    nc = tc.nc
+    with ExitStack() as ctx:
+        keep = ctx.enter_context(tc.tile_pool(name="keep", bufs=1))
+        psum = ctx.enter_context(tc.psum_pool(name="psum", bufs=1))
+
+        offsets = keep.tile([P, D * V // COLS], U16, name="offsets")
+        nc.sync.dma_start(offsets[:], offs)
+
+        w_scale = keep.tile([P, N], U8, name="w_scale", align_bytes=64)
+        nc.vector.memset(w_scale[:].bitcast(I32), 0)
+
+        levels = xT.rearrange("(p l) t -> l p t", l=D)
+        tables = []
+        for l in range(D):
+            table = keep.tile([P, T], F32, name=f"table{l}", align_bytes=64)
+            nc.sync.dma_start(out=table[:], in_=levels[l])
+            tables.append(table)
+
+        w_code = keep.tile([P, N], U32, name="w_code", align_bytes=64)
+        nc.sync.dma_start(out=w_code[:].bitcast(I32), in_=w_words[0].rearrange("p m r -> p (m r)").bitcast(I32))
+        scale_rows = w_scales[0].rearrange("(q r) m -> r q m", r=4)
+        for r in range(4):
+            nc.sync.dma_start(out=w_scale[r:P:32, :].bitcast(I32), in_=scale_rows[r].bitcast(I32))
+
+        def looked_up(l, v0, n):
+            c0 = (l * V + v0) // COLS
+            return tables[l][:].indirect(offsets[:, c0 : c0 + n // COLS])
+
+        early = keep.tile([P, 2, V], F32, name="early", align_bytes=64)
+        grouped = [keep.tile([P, HALF, D], BF16, name=f"grouped{h}", align_bytes=64) for h in range(2)]
+        for l in range(2):
+            nc.vector.tensor_copy(out=early[:, l, :], in_=looked_up(l, 0, V))
+        for h in range(2):
+            nc.scalar.copy(
+                out=grouped[h][:, :, 0:2],
+                in_=early[:, :, h * HALF : (h + 1) * HALF].rearrange("p l v -> p v l"),
+            )
+        for l in range(2, D):
+            for h in range(2):
+                nc.vector.tensor_copy(out=grouped[h][:, :, l], in_=looked_up(l, h * HALF, HALF))
+
+        x_code = [keep.tile([P, HALF], U32, name=f"x_code{h}", align_bytes=64) for h in range(2)]
+        x_scale = [keep.tile([P, HALF], U8, name=f"x_scale{h}", align_bytes=64) for h in range(2)]
+        for h in range(2):
+            nc.vector.quantize_mx(
+                out=x_code[h][:].bitcast(FP8X4),
+                scales=x_scale[h][:],
+                in_=grouped[h][:].rearrange("p v l -> p (v l)"),
+            )
+
+        out_rows = out.rearrange("(j p) v -> p j v", p=P)
+        for h in range(2):
+            for pair in range(2):
+                acc = psum.tile([P, 2, HALF], F32, name=f"acc{h}{pair}")
+                for i in range(2):
+                    cols = slice((2 * pair + i) * P, (2 * pair + i + 1) * P)
+                    nc.tensor.matmul_mx(
+                        out=acc[:, i, :],
+                        lhsT=w_code[:, cols].bitcast(FP8X4),
+                        lhsT_scale=w_scale[:, cols],
+                        rhs=x_code[h][:].bitcast(FP8X4),
+                        rhs_scale=x_scale[h][:],
+                        start=True,
+                        stop=True,
+                    )
+                result = keep.tile([P, 2, HALF], F32, name=f"result{h}{pair}")
+                if pair == 0:
+                    nc.scalar.copy(out=result[:], in_=acc[:])
+                else:
+                    nc.vector.tensor_copy(out=result[:], in_=acc[:])
+                nc.sync.dma_start(
+                    out=out_rows[:, 2 * pair : 2 * pair + 2, h * HALF : (h + 1) * HALF], in_=result[:]
+                )

@@ -25,17 +25,22 @@ def tile_picked_grid_lin_none_sub_l_kernel(tc, xT, w_words, w_scales, offs, out)
         psum = ctx.enter_context(tc.psum_pool(name="psum", bufs=1))
 
         offsets = keep.tile([P, D * V // COLS], U16, name="offsets")
-        nc.sync.dma_start(offsets[:], offs)
 
         w_scale = keep.tile([P, N], U8, name="w_scale", align_bytes=64)
         nc.vector.memset(w_scale[:].bitcast(I32), 0)
 
+        warm = keep.tile([P, 2, 8], F32, name="warm")
+        nc.vector.memset(warm[:, 0, :], 0.0)
+        nc.scalar.copy(out=warm[:, 1, :], in_=warm[:, 0, :])
+
         levels = xT.rearrange("(p l) t -> l p t", l=D)
-        tables = []
-        for l in range(D):
+        tables = {}
+        for l in (2, 0, 1, 3):
             table = keep.tile([P, T], F32, name=f"table{l}", align_bytes=64)
             nc.sync.dma_start(out=table[:], in_=levels[l])
-            tables.append(table)
+            tables[l] = table
+            if l == 2:
+                nc.sync.dma_start(offsets[:], offs)
 
         w_code = keep.tile([P, N], U32, name="w_code", align_bytes=64)
         nc.sync.dma_start(out=w_code[:].bitcast(I32), in_=w_words[0].rearrange("p m r -> p (m r)").bitcast(I32))
@@ -48,17 +53,15 @@ def tile_picked_grid_lin_none_sub_l_kernel(tc, xT, w_words, w_scales, offs, out)
             return tables[l][:].indirect(offsets[:, c0 : c0 + n // COLS])
 
         early = keep.tile([P, 2, V], F32, name="early", align_bytes=64)
-        grouped = [keep.tile([P, HALF, D], BF16, name=f"grouped{h}", align_bytes=64) for h in range(2)]
-        for l in range(2):
-            nc.vector.tensor_copy(out=early[:, l, :], in_=looked_up(l, 0, V))
+        grouped = keep.tile([P, V, D], BF16, name="grouped", align_bytes=64)
+        halves = [slice(h * HALF, (h + 1) * HALF) for h in range(2)]
+        nc.vector.tensor_copy(out=grouped[:, :, 2], in_=looked_up(2, 0, V))
+        nc.vector.tensor_copy(out=early[:, 0, :], in_=looked_up(0, 0, V))
         for h in range(2):
-            nc.scalar.copy(
-                out=grouped[h][:, :, 0:2],
-                in_=early[:, :, h * HALF : (h + 1) * HALF].rearrange("p l v -> p v l"),
-            )
-        for l in range(2, D):
-            for h in range(2):
-                nc.vector.tensor_copy(out=grouped[h][:, :, l], in_=looked_up(l, h * HALF, HALF))
+            nc.vector.tensor_copy(out=early[:, 1, halves[h]], in_=looked_up(1, h * HALF, HALF))
+            nc.scalar.copy(out=grouped[:, halves[h], 0:2], in_=early[:, :, halves[h]].rearrange("p l v -> p v l"))
+        for h in range(2):
+            nc.vector.tensor_copy(out=grouped[:, halves[h], 3], in_=looked_up(3, h * HALF, HALF))
 
         x_code = [keep.tile([P, HALF], U32, name=f"x_code{h}", align_bytes=64) for h in range(2)]
         x_scale = [keep.tile([P, HALF], U8, name=f"x_scale{h}", align_bytes=64) for h in range(2)]
@@ -66,17 +69,18 @@ def tile_picked_grid_lin_none_sub_l_kernel(tc, xT, w_words, w_scales, offs, out)
             nc.vector.quantize_mx(
                 out=x_code[h][:].bitcast(FP8X4),
                 scales=x_scale[h][:],
-                in_=grouped[h][:].rearrange("p v l -> p (v l)"),
+                in_=grouped[:, halves[h], :].rearrange("p v l -> p (v l)"),
             )
 
         out_rows = out.rearrange("(j p) v -> p j v", p=P)
         for h in range(2):
             for pair in range(2):
-                acc = psum.tile([P, 2, HALF], F32, name=f"acc{h}{pair}")
+                result = keep.tile([P, 2, HALF], F32, name=f"result{h}{pair}")
                 for i in range(2):
                     cols = slice((2 * pair + i) * P, (2 * pair + i + 1) * P)
+                    acc = psum.tile([P, HALF], F32, name=f"acc{h}{pair}{i}")
                     nc.tensor.matmul_mx(
-                        out=acc[:, i, :],
+                        out=acc[:],
                         lhsT=w_code[:, cols].bitcast(FP8X4),
                         lhsT_scale=w_scale[:, cols],
                         rhs=x_code[h][:].bitcast(FP8X4),
@@ -84,11 +88,10 @@ def tile_picked_grid_lin_none_sub_l_kernel(tc, xT, w_words, w_scales, offs, out)
                         start=True,
                         stop=True,
                     )
-                result = keep.tile([P, 2, HALF], F32, name=f"result{h}{pair}")
-                if pair == 0:
-                    nc.scalar.copy(out=result[:], in_=acc[:])
-                else:
-                    nc.vector.tensor_copy(out=result[:], in_=acc[:])
+                    if i == 0:
+                        nc.scalar.copy(out=result[:, i, :], in_=acc[:])
+                    else:
+                        nc.vector.tensor_copy(out=result[:, i, :], in_=acc[:])
                 nc.sync.dma_start(
                     out=out_rows[:, 2 * pair : 2 * pair + 2, h * HALF : (h + 1) * HALF], in_=result[:]
                 )

@@ -63,35 +63,38 @@ def tile_picked_grid_lin_none_sub_l_kernel(tc, xT, w_words, w_scales, offs, out)
         for h in range(2):
             nc.vector.tensor_copy(out=grouped[:, halves[h], 3], in_=looked_up(3, h * HALF, HALF))
 
-        x_code = [keep.tile([P, HALF], U32, name=f"x_code{h}", align_bytes=64) for h in range(2)]
-        x_scale = [keep.tile([P, HALF], U8, name=f"x_scale{h}", align_bytes=64) for h in range(2)]
-        for h in range(2):
+        x_code = keep.tile([P, V], U32, name="x_code", align_bytes=64)
+        x_scale = keep.tile([P, V], U8, name="x_scale", align_bytes=64)
+        for points in halves:
             nc.vector.quantize_mx(
-                out=x_code[h][:].bitcast(FP8X4),
-                scales=x_scale[h][:],
-                in_=grouped[:, halves[h], :].rearrange("p v l -> p (v l)"),
+                out=x_code[:, points].bitcast(FP8X4),
+                scales=x_scale[:, points],
+                in_=grouped[:, points, :].rearrange("p v l -> p (v l)"),
             )
 
-        out_rows = out.rearrange("(j p) v -> p j v", p=P)
-        for h in range(2):
-            for pair in range(2):
-                result = keep.tile([P, 2, HALF], F32, name=f"result{h}{pair}")
-                for i in range(2):
-                    cols = slice((2 * pair + i) * P, (2 * pair + i + 1) * P)
-                    acc = psum.tile([P, HALF], F32, name=f"acc{h}{pair}{i}")
-                    nc.tensor.matmul_mx(
-                        out=acc[:],
-                        lhsT=w_code[:, cols].bitcast(FP8X4),
-                        lhsT_scale=w_scale[:, cols],
-                        rhs=x_code[h][:].bitcast(FP8X4),
-                        rhs_scale=x_scale[h][:],
-                        start=True,
-                        stop=True,
-                    )
-                    if i == 0:
-                        nc.scalar.copy(out=result[:, i, :], in_=acc[:])
-                    else:
-                        nc.vector.tensor_copy(out=result[:, i, :], in_=acc[:])
-                nc.sync.dma_start(
-                    out=out_rows[:, 2 * pair : 2 * pair + 2, h * HALF : (h + 1) * HALF], in_=result[:]
-                )
+        def product(j, points, dest, on_scalar):
+            cols = slice(j * P, (j + 1) * P)
+            acc = psum.tile([P, points.stop - points.start], F32, name=f"acc{j}_{points.start}")
+            nc.tensor.matmul_mx(
+                out=acc[:],
+                lhsT=w_code[:, cols].bitcast(FP8X4),
+                lhsT_scale=w_scale[:, cols],
+                rhs=x_code[:, points].bitcast(FP8X4),
+                rhs_scale=x_scale[:, points],
+                start=True,
+                stop=True,
+            )
+            if on_scalar:
+                nc.scalar.copy(out=dest, in_=acc[:])
+            else:
+                nc.vector.tensor_copy(out=dest, in_=acc[:])
+
+        result = keep.tile([P, D, V], F32, name="result")
+        order = [(0, 0), (1, 0), (0, 1), (1, 1), (2, 0), (2, 1), (3, 0), (3, 1)]
+        for step, (j, h) in enumerate(order):
+            product(j, halves[h], result[:, j, halves[h]], step % 2 == 0)
+            rows = slice(j * P, (j + 1) * P)
+            if j == 0:
+                nc.sync.dma_start(out=out[rows, halves[h]], in_=result[:, j, halves[h]])
+            elif h == 1:
+                nc.sync.dma_start(out=out[rows, :], in_=result[:, j, :])

@@ -42,11 +42,13 @@ def tile_picked_grid_lin_none_sub_l_kernel(tc, xT, w_words, w_scales, offs, out)
             if l == 2:
                 nc.sync.dma_start(offsets[:], offs)
 
-        w_code = keep.tile([P, N], U32, name="w_code", align_bytes=64)
-        nc.sync.dma_start(out=w_code[:].bitcast(I32), in_=w_words[0].rearrange("p m r -> p (m r)").bitcast(I32))
         scale_rows = w_scales[0].rearrange("(q r) m -> r q m", r=4)
         for r in range(4):
             nc.sync.dma_start(out=w_scale[r:P:32, :].bitcast(I32), in_=scale_rows[r].bitcast(I32))
+        w_code = keep.tile([P, N], U32, name="w_code", align_bytes=64)
+        w_rows = w_words[0].rearrange("p m r -> p (m r)").bitcast(I32)
+        for cols in (slice(0, N // 2), slice(N // 2, N)):
+            nc.sync.dma_start(out=w_code[:, cols].bitcast(I32), in_=w_rows[:, cols])
 
         def looked_up(l, v0, n):
             c0 = (l * V + v0) // COLS

@@ -54,25 +54,30 @@ def tile_picked_grid_lin_none_sub_l_kernel(tc, xT, w_words, w_scales, offs, out)
             c0 = (l * V + v0) // COLS
             return tables[l][:].indirect(offsets[:, c0 : c0 + n // COLS])
 
-        early = keep.tile([P, 2, V], F32, name="early", align_bytes=64)
-        grouped = keep.tile([P, V, D], BF16, name="grouped", align_bytes=64)
         halves = [slice(h * HALF, (h + 1) * HALF) for h in range(2)]
-        nc.vector.tensor_copy(out=grouped[:, :, 2], in_=looked_up(2, 0, V))
+        grouped = keep.tile([P, V, D], BF16, name="grouped", align_bytes=64)
+        x_code = keep.tile([P, V], U32, name="x_code", align_bytes=64)
+        x_scale = keep.tile([P, V], U8, name="x_scale", align_bytes=64)
+
+        def quantise(v0, v1):
+            nc.vector.quantize_mx(
+                out=x_code[:, v0:v1].bitcast(FP8X4),
+                scales=x_scale[:, v0:v1],
+                in_=grouped[:, v0:v1, :].rearrange("p v l -> p (v l)"),
+            )
+
+        early = keep.tile([P, 3, V], F32, name="early", align_bytes=64)
+        nc.vector.tensor_copy(out=early[:, 2, :], in_=looked_up(2, 0, V))
+        for points in halves:
+            nc.scalar.copy(out=grouped[:, points, 2:4], in_=early[:, 2, points].unsqueeze(2).to_broadcast([P, HALF, 2]))
         nc.vector.tensor_copy(out=early[:, 0, :], in_=looked_up(0, 0, V))
         for h in range(2):
             nc.vector.tensor_copy(out=early[:, 1, halves[h]], in_=looked_up(1, h * HALF, HALF))
-            nc.scalar.copy(out=grouped[:, halves[h], 0:2], in_=early[:, :, halves[h]].rearrange("p l v -> p v l"))
-        for h in range(2):
-            nc.vector.tensor_copy(out=grouped[:, halves[h], 3], in_=looked_up(3, h * HALF, HALF))
-
-        x_code = keep.tile([P, V], U32, name="x_code", align_bytes=64)
-        x_scale = keep.tile([P, V], U8, name="x_scale", align_bytes=64)
-        for points in halves:
-            nc.vector.quantize_mx(
-                out=x_code[:, points].bitcast(FP8X4),
-                scales=x_scale[:, points],
-                in_=grouped[:, points, :].rearrange("p v l -> p (v l)"),
-            )
+            nc.scalar.copy(out=grouped[:, halves[h], 0:2], in_=early[:, 0:2, halves[h]].rearrange("p l v -> p v l"))
+        for v0, v1 in ((0, 128), (128, 192), (192, 256)):
+            nc.vector.tensor_copy(out=grouped[:, v0:v1, 3], in_=looked_up(3, v0, v1 - v0))
+        for v0, v1 in ((0, 128), (128, 192), (192, 256)):
+            quantise(v0, v1)
 
         def product(j, points, dest, on_scalar):
             cols = slice(j * P, (j + 1) * P)
@@ -92,11 +97,11 @@ def tile_picked_grid_lin_none_sub_l_kernel(tc, xT, w_words, w_scales, offs, out)
                 nc.vector.tensor_copy(out=dest, in_=acc[:])
 
         result = keep.tile([P, D, V], F32, name="result")
-        order = [(0, 0), (1, 0), (0, 1), (1, 1), (2, 0), (2, 1), (3, 0), (3, 1)]
-        for step, (j, h) in enumerate(order):
-            product(j, halves[h], result[:, j, halves[h]], step % 2 == 0)
+        for j in range(4):
             rows = slice(j * P, (j + 1) * P)
-            if j == 0:
-                nc.sync.dma_start(out=out[rows, halves[h]], in_=result[:, j, halves[h]])
-            elif h == 1:
+            for h in range(2):
+                product(j, halves[h], result[:, j, halves[h]], h == 1 and j < 3)
+                if j == 0:
+                    nc.sync.dma_start(out=out[rows, halves[h]], in_=result[:, j, halves[h]])
+            if j > 0:
                 nc.sync.dma_start(out=out[rows, :], in_=result[:, j, :])

@@ -29,10 +29,6 @@ def tile_picked_grid_lin_none_sub_l_kernel(tc, xT, w_words, w_scales, offs, out)
         w_scale = keep.tile([P, N], U8, name="w_scale", align_bytes=64)
         nc.vector.memset(w_scale[:].bitcast(I32), 0)
 
-        warm = keep.tile([P, 2, 8], F32, name="warm")
-        nc.vector.memset(warm[:, 0, :], 0.0)
-        nc.scalar.copy(out=warm[:, 1, :], in_=warm[:, 0, :])
-
         levels = xT.rearrange("(p l) t -> l p t", l=D)
         tables = {}
         for l in (2, 0, 1, 3):
@@ -99,9 +95,11 @@ def tile_picked_grid_lin_none_sub_l_kernel(tc, xT, w_words, w_scales, offs, out)
         result = keep.tile([P, D, V], F32, name="result")
         for j in range(4):
             rows = slice(j * P, (j + 1) * P)
-            for h in range(2):
-                product(j, halves[h], result[:, j, halves[h]], h == 1 and j < 3)
-                if j == 0:
-                    nc.sync.dma_start(out=out[rows, halves[h]], in_=result[:, j, halves[h]])
-            if j > 0:
-                nc.sync.dma_start(out=out[rows, :], in_=result[:, j, :])
+            scalar_ends = j % 2 == 0
+            last_queue = nc.scalar if scalar_ends else nc.sync
+            product(j, halves[0], result[:, j, halves[0]], False)
+            if j == 0:
+                nc.sync.dma_start(out=out[rows, halves[0]], in_=result[:, j, halves[0]])
+            product(j, halves[1], result[:, j, halves[1]], scalar_ends)
+            points = halves[1] if j == 0 else slice(0, V)
+            last_queue.dma_start(out=out[rows, points], in_=result[:, j, points])

@@ -43,7 +43,7 @@ def tile_picked_grid_lin_none_sub_l_kernel(tc, xT, w_words, w_scales, offs, out)
             nc.sync.dma_start(out=w_scale[r:P:32, :].bitcast(I32), in_=scale_rows[r].bitcast(I32))
         w_code = keep.tile([P, N], U32, name="w_code", align_bytes=64)
         w_rows = w_words[0].rearrange("p m r -> p (m r)").bitcast(I32)
-        for cols in (slice(0, N // 2), slice(N // 2, N)):
+        for cols in (slice(0, P), slice(P, N)):
             nc.sync.dma_start(out=w_code[:, cols].bitcast(I32), in_=w_rows[:, cols])
 
         def looked_up(l, v0, n):

@@ -12,6 +12,7 @@ U32 = mybir.dt.uint32
 U16 = mybir.dt.uint16
 U8 = mybir.dt.uint8
 FP8X4 = mybir.dt.float8_e4m3fn_x4
+COPY = mybir.ActivationFunctionType.Copy
 
 P = 128
 HALF = V // 2
@@ -25,17 +26,18 @@ def tile_picked_grid_lin_none_sub_l_kernel(tc, xT, w_words, w_scales, offs, out)
         psum = ctx.enter_context(tc.psum_pool(name="psum", bufs=1))
 
         offsets = keep.tile([P, D * V // COLS], U16, name="offsets")
-
         w_scale = keep.tile([P, N], U8, name="w_scale", align_bytes=64)
-        nc.vector.memset(w_scale[:].bitcast(I32), 0)
+        zeros = w_scale[:].bitcast(U32)
+        nc.vector.memset(zeros[:, : N // 8], 0)
+        nc.scalar.copy(out=zeros[:, N // 8 :], in_=zeros[:, : N // 8])
 
         levels = xT.rearrange("(p l) t -> l p t", l=D)
-        tables = {}
-        for l in (2, 0, 1, 3):
+        tables = []
+        for l in range(D):
             table = keep.tile([P, T], F32, name=f"table{l}", align_bytes=64)
             nc.sync.dma_start(out=table[:], in_=levels[l])
-            tables[l] = table
-            if l == 2:
+            tables.append(table)
+            if l == 0:
                 nc.sync.dma_start(offsets[:], offs)
 
         scale_rows = w_scales[0].rearrange("(q r) m -> r q m", r=4)
@@ -50,56 +52,71 @@ def tile_picked_grid_lin_none_sub_l_kernel(tc, xT, w_words, w_scales, offs, out)
             c0 = (l * V + v0) // COLS
             return tables[l][:].indirect(offsets[:, c0 : c0 + n // COLS])
 
-        halves = [slice(h * HALF, (h + 1) * HALF) for h in range(2)]
-        grouped = keep.tile([P, V, D], BF16, name="grouped", align_bytes=64)
-        x_code = keep.tile([P, V], U32, name="x_code", align_bytes=64)
-        x_scale = keep.tile([P, V], U8, name="x_scale", align_bytes=64)
+        grouped = [keep.tile([P, HALF, D], BF16, name=f"grouped{h}", align_bytes=64) for h in range(2)]
+        x_scale = [keep.tile([P, HALF], U8, name=f"x_scale{h}", align_bytes=64) for h in range(2)]
+        QUARTER = HALF // 2
+        early = keep.tile([P, 2, HALF], BF16, name="early", align_bytes=64)
+        late = [keep.tile([P, 2, QUARTER], BF16, name=f"late{q}", tag=f"late{q}", align_bytes=64) for q in range(2)]
 
-        def quantise(v0, v1):
-            nc.vector.quantize_mx(
-                out=x_code[:, v0:v1].bitcast(FP8X4),
-                scales=x_scale[:, v0:v1],
-                in_=grouped[:, v0:v1, :].rearrange("p v l -> p (v l)"),
+        def lay(w, v0, pairs):
+            nc.vector.tensor_copy(
+                out=grouped[1][:, v0 : v0 + pairs.shape[2], 2 * w : 2 * w + 2],
+                in_=pairs[:].rearrange("p l v -> p v l"),
             )
 
-        early = keep.tile([P, 3, V], F32, name="early", align_bytes=64)
-        nc.vector.tensor_copy(out=early[:, 2, :], in_=looked_up(2, 0, V))
-        for points in halves:
-            nc.scalar.copy(out=grouped[:, points, 2:4], in_=early[:, 2, points].unsqueeze(2).to_broadcast([P, HALF, 2]))
-        nc.vector.tensor_copy(out=early[:, 0, :], in_=looked_up(0, 0, V))
+        for l in range(D):
+            nc.vector.tensor_copy(out=grouped[0][:, :, l], in_=looked_up(l, 0, HALF))
+            if l < 2:
+                nc.scalar.activation(early[:, l, :], looked_up(l, HALF, HALF), COPY)
+            else:
+                for q in range(2):
+                    nc.scalar.activation(late[q][:, l % 2, :], looked_up(l, HALF + q * QUARTER, QUARTER), COPY)
+            if l == 1:
+                lay(0, 0, early)
+        for q in range(2):
+            lay(1, q * QUARTER, late[q])
+        x_code = [keep.tile([P, HALF], U32, name=f"x_code{h}", tag=("late0", "x_code1")[h], align_bytes=64) for h in range(2)]
         for h in range(2):
-            nc.vector.tensor_copy(out=early[:, 1, halves[h]], in_=looked_up(1, h * HALF, HALF))
-            nc.scalar.copy(out=grouped[:, halves[h], 0:2], in_=early[:, 0:2, halves[h]].rearrange("p l v -> p v l"))
-        for v0, v1 in ((0, 128), (128, 192), (192, 256)):
-            nc.vector.tensor_copy(out=grouped[:, v0:v1, 3], in_=looked_up(3, v0, v1 - v0))
-        for v0, v1 in ((0, 128), (128, 192), (192, 256)):
-            quantise(v0, v1)
+            nc.vector.quantize_mx(
+                out=x_code[h][:].bitcast(FP8X4),
+                scales=x_scale[h][:],
+                in_=grouped[h][:].rearrange("p v l -> p (v l)"),
+            )
 
-        def product(j, points, dest, on_scalar):
+        halves = [slice(h * HALF, (h + 1) * HALF) for h in range(2)]
+        result = keep.tile([P, D, V], F32, name="result")
+
+        def product(j, h, on_scalar):
             cols = slice(j * P, (j + 1) * P)
-            acc = psum.tile([P, points.stop - points.start], F32, name=f"acc{j}_{points.start}")
+            acc = psum.tile([P, HALF], F32, name=f"acc{j}_{h}")
             nc.tensor.matmul_mx(
                 out=acc[:],
                 lhsT=w_code[:, cols].bitcast(FP8X4),
                 lhsT_scale=w_scale[:, cols],
-                rhs=x_code[:, points].bitcast(FP8X4),
-                rhs_scale=x_scale[:, points],
+                rhs=x_code[h][:].bitcast(FP8X4),
+                rhs_scale=x_scale[h][:],
                 start=True,
                 stop=True,
             )
             if on_scalar:
-                nc.scalar.copy(out=dest, in_=acc[:])
+                nc.scalar.copy(out=result[:, j, halves[h]], in_=acc[:])
             else:
-                nc.vector.tensor_copy(out=dest, in_=acc[:])
+                nc.vector.tensor_copy(out=result[:, j, halves[h]], in_=acc[:])
 
-        result = keep.tile([P, D, V], F32, name="result")
-        for j in range(4):
-            rows = slice(j * P, (j + 1) * P)
-            scalar_ends = j % 2 == 0
-            last_queue = nc.scalar if scalar_ends else nc.sync
-            product(j, halves[0], result[:, j, halves[0]], False)
-            if j == 0:
-                nc.sync.dma_start(out=out[rows, halves[0]], in_=result[:, j, halves[0]])
-            product(j, halves[1], result[:, j, halves[1]], scalar_ends)
-            points = halves[1] if j == 0 else slice(0, V)
-            last_queue.dma_start(out=out[rows, points], in_=result[:, j, points])
+        def store(j, points, queue):
+            queue.dma_start(out=out[j * P : (j + 1) * P, points], in_=result[:, j, points])
+
+        whole = slice(0, V)
+        product(0, 0, True)
+        store(0, halves[0], nc.sync)
+        product(1, 0, False)
+        product(0, 1, True)
+        store(0, halves[1], nc.scalar)
+        product(1, 1, False)
+        store(1, whole, nc.sync)
+        product(2, 0, False)
+        product(2, 1, True)
+        store(2, whole, nc.scalar)
+        product(3, 0, False)
+        product(3, 1, False)
+        store(3, whole, nc.sync)

@@ -40,47 +40,53 @@ def tile_picked_grid_lin_none_sub_l_kernel(tc, xT, w_words, w_scales, offs, out)
             if l == 0:
                 nc.sync.dma_start(offsets[:], offs)
 
+        w_code = keep.tile([P, N], U32, name="w_code", align_bytes=64)
+        w_rows = w_words[0].rearrange("p m r -> p (m r)").bitcast(I32)
+        nc.sync.dma_start(out=w_code[:, : N // 2].bitcast(I32), in_=w_rows[:, : N // 2])
         scale_rows = w_scales[0].rearrange("(q r) m -> r q m", r=4)
         for r in range(4):
             nc.sync.dma_start(out=w_scale[r:P:32, :].bitcast(I32), in_=scale_rows[r].bitcast(I32))
-        w_code = keep.tile([P, N], U32, name="w_code", align_bytes=64)
-        w_rows = w_words[0].rearrange("p m r -> p (m r)").bitcast(I32)
-        for cols in (slice(0, P), slice(P, N)):
-            nc.sync.dma_start(out=w_code[:, cols].bitcast(I32), in_=w_rows[:, cols])
+        nc.sync.dma_start(out=w_code[:, N // 2 :].bitcast(I32), in_=w_rows[:, N // 2 :])
 
         def looked_up(l, v0, n):
             c0 = (l * V + v0) // COLS
             return tables[l][:].indirect(offsets[:, c0 : c0 + n // COLS])
 
-        grouped = [keep.tile([P, HALF, D], BF16, name=f"grouped{h}", align_bytes=64) for h in range(2)]
-        x_scale = [keep.tile([P, HALF], U8, name=f"x_scale{h}", align_bytes=64) for h in range(2)]
         QUARTER = HALF // 2
-        early = keep.tile([P, 2, HALF], BF16, name="early", align_bytes=64)
-        late = [keep.tile([P, 2, QUARTER], BF16, name=f"late{q}", tag=f"late{q}", align_bytes=64) for q in range(2)]
+        third, fourth = slice(HALF, HALF + QUARTER), slice(HALF + QUARTER, V)
+        grouped = keep.tile([P, V, D], BF16, name="grouped", align_bytes=64)
+        x_code = [keep.tile([P, HALF], U32, name=f"x_code{h}", align_bytes=64) for h in range(2)]
+        x_scale = [keep.tile([P, HALF], U8, name=f"x_scale{h}", align_bytes=64) for h in range(2)]
+        dense_third = keep.tile([P, 2, QUARTER], BF16, name="dense_third", align_bytes=64)
+        dense_fourth = [keep.tile([P, 2, QUARTER], BF16, name=f"dense_fourth{w}", align_bytes=64) for w in range(2)]
 
-        def lay(w, v0, pairs):
-            nc.vector.tensor_copy(
-                out=grouped[1][:, v0 : v0 + pairs.shape[2], 2 * w : 2 * w + 2],
-                in_=pairs[:].rearrange("p l v -> p v l"),
-            )
+        def into_place(l, points):
+            nc.vector.tensor_copy(out=grouped[:, points, l], in_=looked_up(l, points.start, points.stop - points.start))
 
-        for l in range(D):
-            nc.vector.tensor_copy(out=grouped[0][:, :, l], in_=looked_up(l, 0, HALF))
-            if l < 2:
-                nc.scalar.activation(early[:, l, :], looked_up(l, HALF, HALF), COPY)
-            else:
-                for q in range(2):
-                    nc.scalar.activation(late[q][:, l % 2, :], looked_up(l, HALF + q * QUARTER, QUARTER), COPY)
-            if l == 1:
-                lay(0, 0, early)
-        for q in range(2):
-            lay(1, q * QUARTER, late[q])
-        x_code = [keep.tile([P, HALF], U32, name=f"x_code{h}", tag=("late0", "x_code1")[h], align_bytes=64) for h in range(2)]
-        for h in range(2):
+        def dense(l, points, pairs):
+            nc.scalar.activation(pairs[:, l % 2, :], looked_up(l, points.start, QUARTER), COPY)
+
+        def by_point(pairs):
+            return pairs[:].rearrange("p l v -> p v l")
+
+        for l in (0, 1):
+            into_place(l, slice(0, HALF))
+            dense(l, third, dense_third)
+            dense(l, fourth, dense_fourth[0])
+        nc.vector.tensor_copy(out=grouped[:, third, 0:2], in_=by_point(dense_third))
+        into_place(2, slice(0, HALF + QUARTER))
+        dense(2, fourth, dense_fourth[1])
+        nc.scalar.copy(out=grouped[:, fourth, 0:2], in_=by_point(dense_fourth[0]))
+        into_place(3, slice(0, HALF))
+        into_place(3, third)
+        dense(3, fourth, dense_fourth[1])
+        nc.scalar.copy(out=grouped[:, fourth, 2:4], in_=by_point(dense_fourth[1]))
+        for points in (slice(0, HALF), third, fourth):
+            h, cols = points.start // HALF, slice(points.start % HALF, (points.stop - 1) % HALF + 1)
             nc.vector.quantize_mx(
-                out=x_code[h][:].bitcast(FP8X4),
-                scales=x_scale[h][:],
-                in_=grouped[h][:].rearrange("p v l -> p (v l)"),
+                out=x_code[h][:, cols].bitcast(FP8X4),
+                scales=x_scale[h][:, cols],
+                in_=grouped[:, points, :].rearrange("p v l -> p (v l)"),
             )
 
         halves = [slice(h * HALF, (h + 1) * HALF) for h in range(2)]

@@ -109,20 +109,17 @@ def tile_picked_grid_lin_none_sub_l_kernel(tc, xT, w_words, w_scales, offs, out)
             else:
                 nc.vector.tensor_copy(out=result[:, j, halves[h]], in_=acc[:])
 
-        def store(j, points, queue):
-            queue.dma_start(out=out[j * P : (j + 1) * P, points], in_=result[:, j, points])
+        def store(j, points):
+            nc.sync.dma_start(out=out[j * P : (j + 1) * P, points], in_=result[:, j, points])
 
-        whole = slice(0, V)
-        product(0, 0, True)
-        store(0, halves[0], nc.sync)
-        product(1, 0, False)
-        product(0, 1, True)
-        store(0, halves[1], nc.scalar)
+        product(0, 0, False)
+        store(0, halves[0])
+        product(1, 0, True)
+        product(0, 1, False)
+        store(0, halves[1])
         product(1, 1, False)
-        store(1, whole, nc.sync)
-        product(2, 0, False)
-        product(2, 1, True)
-        store(2, whole, nc.scalar)
-        product(3, 0, False)
-        product(3, 1, False)
-        store(3, whole, nc.sync)
+        store(1, slice(0, V))
+        for j in (2, 3):
+            product(j, 0, True)
+            product(j, 1, False)
+            store(j, slice(0, V))

@@ -57,29 +57,30 @@ def tile_picked_grid_lin_none_sub_l_kernel(tc, xT, w_words, w_scales, offs, out)
         grouped = keep.tile([P, V, D], BF16, name="grouped", align_bytes=64)
         x_code = [keep.tile([P, HALF], U32, name=f"x_code{h}", align_bytes=64) for h in range(2)]
         x_scale = [keep.tile([P, HALF], U8, name=f"x_scale{h}", align_bytes=64) for h in range(2)]
-        dense_third = keep.tile([P, 2, QUARTER], BF16, name="dense_third", align_bytes=64)
+        dense_third = keep.tile([P, 3, QUARTER], BF16, name="dense_third", align_bytes=64)
         dense_fourth = [keep.tile([P, 2, QUARTER], BF16, name=f"dense_fourth{w}", align_bytes=64) for w in range(2)]
 
         def into_place(l, points):
             nc.vector.tensor_copy(out=grouped[:, points, l], in_=looked_up(l, points.start, points.stop - points.start))
 
-        def dense(l, points, pairs):
-            nc.scalar.activation(pairs[:, l % 2, :], looked_up(l, points.start, QUARTER), COPY)
+        def dense(l, points, row):
+            nc.scalar.activation(row, looked_up(l, points.start, QUARTER), COPY)
 
-        def by_point(pairs):
-            return pairs[:].rearrange("p l v -> p v l")
+        def by_point(rows):
+            return rows[:].rearrange("p l v -> p v l")
 
         for l in (0, 1):
             into_place(l, slice(0, HALF))
-            dense(l, third, dense_third)
-            dense(l, fourth, dense_fourth[0])
-        nc.vector.tensor_copy(out=grouped[:, third, 0:2], in_=by_point(dense_third))
-        into_place(2, slice(0, HALF + QUARTER))
-        dense(2, fourth, dense_fourth[1])
-        nc.scalar.copy(out=grouped[:, fourth, 0:2], in_=by_point(dense_fourth[0]))
+            dense(l, fourth, dense_fourth[0][:, l, :])
+            dense(l, third, dense_third[:, l, :])
+        nc.vector.tensor_copy(out=grouped[:, fourth, 0:2], in_=by_point(dense_fourth[0]))
+        into_place(2, slice(0, HALF))
+        dense(2, third, dense_third[:, 2, :])
+        dense(2, fourth, dense_fourth[1][:, 0, :])
+        nc.vector.tensor_copy(out=grouped[:, third, 0:3], in_=by_point(dense_third))
         into_place(3, slice(0, HALF))
         into_place(3, third)
-        dense(3, fourth, dense_fourth[1])
+        dense(3, fourth, dense_fourth[1][:, 1, :])
         nc.scalar.copy(out=grouped[:, fourth, 2:4], in_=by_point(dense_fourth[1]))
         for points in (slice(0, HALF), third, fourth):
             h, cols = points.start // HALF, slice(points.start % HALF, (points.stop - 1) % HALF + 1)

@@ -93,7 +93,7 @@ def tile_picked_grid_lin_none_sub_l_kernel(tc, xT, w_words, w_scales, offs, out)
         halves = [slice(h * HALF, (h + 1) * HALF) for h in range(2)]
         result = keep.tile([P, D, V], F32, name="result")
 
-        def product(j, h, on_scalar):
+        def product(j, h):
             cols = slice(j * P, (j + 1) * P)
             acc = psum.tile([P, HALF], F32, name=f"acc{j}_{h}")
             nc.tensor.matmul_mx(
@@ -105,22 +105,19 @@ def tile_picked_grid_lin_none_sub_l_kernel(tc, xT, w_words, w_scales, offs, out)
                 start=True,
                 stop=True,
             )
-            if on_scalar:
-                nc.scalar.copy(out=result[:, j, halves[h]], in_=acc[:])
-            else:
-                nc.vector.tensor_copy(out=result[:, j, halves[h]], in_=acc[:])
+            nc.vector.tensor_copy(out=result[:, j, halves[h]], in_=acc[:])
 
-        def store(j, points):
-            nc.sync.dma_start(out=out[j * P : (j + 1) * P, points], in_=result[:, j, points])
+        def store(j, points, queue):
+            queue.dma_start(out=out[j * P : (j + 1) * P, points], in_=result[:, j, points])
 
-        product(0, 0, False)
-        store(0, halves[0])
-        product(1, 0, True)
-        product(0, 1, False)
-        store(0, halves[1])
-        product(1, 1, False)
-        store(1, slice(0, V))
+        product(0, 0)
+        store(0, halves[0], nc.sync)
+        product(1, 0)
+        product(0, 1)
+        store(0, halves[1], nc.scalar)
+        product(1, 1)
+        store(1, slice(0, V), nc.sync)
         for j in (2, 3):
-            product(j, 0, True)
-            product(j, 1, False)
-            store(j, slice(0, V))
+            product(j, 0)
+            product(j, 1)
+            store(j, slice(0, V), (nc.scalar, nc.sync)[j % 2])

@@ -25,8 +25,8 @@ def tile_picked_grid_lin_none_sub_l_kernel(tc, xT, w_words, w_scales, offs, out)
         keep = ctx.enter_context(tc.tile_pool(name="keep", bufs=1))
         psum = ctx.enter_context(tc.psum_pool(name="psum", bufs=1))
 
-        offsets = keep.tile([P, D * V // COLS], U16, name="offsets")
-        w_scale = keep.tile([P, N], U8, name="w_scale", align_bytes=64)
+        offsets = keep.tile([P, D * V // COLS], U16, name="offsets", align_bytes=256)
+        w_scale = keep.tile([P, N], U8, name="w_scale", align_bytes=256)
         zeros = w_scale[:].bitcast(U32)
         nc.vector.memset(zeros[:, : N // 8], 0)
         nc.scalar.copy(out=zeros[:, N // 8 :], in_=zeros[:, : N // 8])
@@ -34,13 +34,13 @@ def tile_picked_grid_lin_none_sub_l_kernel(tc, xT, w_words, w_scales, offs, out)
         levels = xT.rearrange("(p l) t -> l p t", l=D)
         tables = []
         for l in range(D):
-            table = keep.tile([P, T], F32, name=f"table{l}", align_bytes=64)
+            table = keep.tile([P, T], F32, name=f"table{l}", align_bytes=256)
             nc.sync.dma_start(out=table[:], in_=levels[l])
             tables.append(table)
             if l == 0:
                 nc.sync.dma_start(offsets[:], offs)
 
-        w_code = keep.tile([P, N], U32, name="w_code", align_bytes=64)
+        w_code = keep.tile([P, N], U32, name="w_code", align_bytes=256)
         w_rows = w_words[0].rearrange("p m r -> p (m r)").bitcast(I32)
         nc.sync.dma_start(out=w_code[:, : N // 2].bitcast(I32), in_=w_rows[:, : N // 2])
         scale_rows = w_scales[0].rearrange("(q r) m -> r q m", r=4)
@@ -91,7 +91,7 @@ def tile_picked_grid_lin_none_sub_l_kernel(tc, xT, w_words, w_scales, offs, out)
             )
 
         halves = [slice(h * HALF, (h + 1) * HALF) for h in range(2)]
-        result = keep.tile([P, D, V], F32, name="result")
+        result = keep.tile([P, D, V], F32, name="result", align_bytes=256)
 
         def product(j, h):
             cols = slice(j * P, (j + 1) * P)

@@ -107,17 +107,19 @@ def tile_picked_grid_lin_none_sub_l_kernel(tc, xT, w_words, w_scales, offs, out)
             )
             nc.vector.tensor_copy(out=result[:, j, halves[h]], in_=acc[:])
 
-        def store(j, points, queue):
-            queue.dma_start(out=out[j * P : (j + 1) * P, points], in_=result[:, j, points])
+        out_blocks = out.rearrange("(j p) v -> p j v", p=P)
+
+        def store(blocks, h, queue):
+            queue.dma_start(out=out_blocks[:, blocks, halves[h]], in_=result[:, blocks, halves[h]])
 
         product(0, 0)
-        store(0, halves[0], nc.sync)
+        store(slice(0, 1), 0, nc.sync)
         product(1, 0)
-        product(0, 1)
-        store(0, halves[1], nc.scalar)
-        product(1, 1)
-        store(1, slice(0, V), nc.sync)
-        for j in (2, 3):
-            product(j, 0)
-            product(j, 1)
-            store(j, slice(0, V), (nc.scalar, nc.sync)[j % 2])
+        store(slice(1, 2), 0, nc.scalar)
+        product(2, 0)
+        product(3, 0)
+        store(slice(2, 4), 0, nc.sync)
+        for pair, queue in ((0, nc.scalar), (2, nc.sync)):
+            product(pair, 1)
+            product(pair + 1, 1)
+            store(slice(pair, pair + 2), 1, queue)

@@ -26,10 +26,10 @@ def tile_picked_grid_lin_none_sub_l_kernel(tc, xT, w_words, w_scales, offs, out)
         psum = ctx.enter_context(tc.psum_pool(name="psum", bufs=1))
 
         offsets = keep.tile([P, D * V // COLS], U16, name="offsets", align_bytes=256)
-        w_scale = keep.tile([P, N], U8, name="w_scale", align_bytes=256)
+        w_scale = keep.tile([P, P], U8, name="w_scale", align_bytes=256)
         zeros = w_scale[:].bitcast(U32)
-        nc.vector.memset(zeros[:, : N // 8], 0)
-        nc.scalar.copy(out=zeros[:, N // 8 :], in_=zeros[:, : N // 8])
+        nc.vector.memset(zeros[:, : P // 8], 0)
+        nc.scalar.copy(out=zeros[:, P // 8 :], in_=zeros[:, : P // 8])
 
         levels = xT.rearrange("(p l) t -> l p t", l=D)
         tables = []
@@ -43,9 +43,9 @@ def tile_picked_grid_lin_none_sub_l_kernel(tc, xT, w_words, w_scales, offs, out)
         w_code = keep.tile([P, N], U32, name="w_code", align_bytes=256)
         w_rows = w_words[0].rearrange("p m r -> p (m r)").bitcast(I32)
         nc.sync.dma_start(out=w_code[:, : N // 2].bitcast(I32), in_=w_rows[:, : N // 2])
-        scale_rows = w_scales[0].rearrange("(q r) m -> r q m", r=4)
-        for r in range(4):
-            nc.sync.dma_start(out=w_scale[r:P:32, :].bitcast(I32), in_=scale_rows[r].bitcast(I32))
+        scale_rows = w_scales[0].bitcast(I32).rearrange("(q r) (j m) -> q j r m", r=4, j=D)
+        for q in range(4):
+            nc.sync.dma_start(out=w_scale[32 * q : 32 * q + 16, :].bitcast(I32), in_=scale_rows[q])
         nc.sync.dma_start(out=w_code[:, N // 2 :].bitcast(I32), in_=w_rows[:, N // 2 :])
 
         def looked_up(l, v0, n):
@@ -99,7 +99,7 @@ def tile_picked_grid_lin_none_sub_l_kernel(tc, xT, w_words, w_scales, offs, out)
             nc.tensor.matmul_mx(
                 out=acc[:],
                 lhsT=w_code[:, cols].bitcast(FP8X4),
-                lhsT_scale=w_scale[:, cols],
+                lhsT_scale=w_scale[4 * j :, :],
                 rhs=x_code[h][:].bitcast(FP8X4),
                 rhs_scale=x_scale[h][:],
                 start=True,

from contextlib import ExitStack

import concourse.mybir as mybir

K, T, D, V, N = 512, 512, 4, 256, 512
FLOPS = 2 * K * N * V

F32 = mybir.dt.float32
BF16 = mybir.dt.bfloat16
I32 = mybir.dt.int32
U32 = mybir.dt.uint32
U16 = mybir.dt.uint16
U8 = mybir.dt.uint8
FP8X4 = mybir.dt.float8_e4m3fn_x4
COPY = mybir.ActivationFunctionType.Copy

P = 128
HALF = V // 2
COLS = 16


def tile_picked_grid_lin_none_sub_l_kernel(tc, xT, w_words, w_scales, offs, out):
    nc = tc.nc
    with ExitStack() as ctx:
        keep = ctx.enter_context(tc.tile_pool(name="keep", bufs=1))
        psum = ctx.enter_context(tc.psum_pool(name="psum", bufs=1))

        offsets = keep.tile([P, D * V // COLS], U16, name="offsets", align_bytes=256)
        w_scale = keep.tile([P, P], U8, name="w_scale", align_bytes=256)
        zeros = w_scale[:].bitcast(U32)
        nc.vector.memset(zeros[:, : P // 8], 0)
        nc.scalar.copy(out=zeros[:, P // 8 :], in_=zeros[:, : P // 8])

        levels = xT.rearrange("(p l) t -> l p t", l=D)
        tables = []
        for l in range(D):
            table = keep.tile([P, T], F32, name=f"table{l}", align_bytes=256)
            nc.sync.dma_start(out=table[:], in_=levels[l])
            tables.append(table)
            if l == 0:
                nc.sync.dma_start(offsets[:], offs)

        w_code = keep.tile([P, N], U32, name="w_code", align_bytes=256)
        w_rows = w_words[0].rearrange("p m r -> p (m r)").bitcast(I32)
        nc.sync.dma_start(out=w_code[:, : N // 2].bitcast(I32), in_=w_rows[:, : N // 2])
        scale_rows = w_scales[0].bitcast(I32).rearrange("(q r) (j m) -> q j r m", r=4, j=D)
        for q in range(4):
            nc.sync.dma_start(out=w_scale[32 * q : 32 * q + 16, :].bitcast(I32), in_=scale_rows[q])
        nc.sync.dma_start(out=w_code[:, N // 2 :].bitcast(I32), in_=w_rows[:, N // 2 :])

        def looked_up(l, v0, n):
            c0 = (l * V + v0) // COLS
            return tables[l][:].indirect(offsets[:, c0 : c0 + n // COLS])

        QUARTER = HALF // 2
        third, fourth = slice(HALF, HALF + QUARTER), slice(HALF + QUARTER, V)
        grouped = keep.tile([P, V, D], BF16, name="grouped", align_bytes=64)
        x_code = [keep.tile([P, HALF], U32, name=f"x_code{h}", align_bytes=64) for h in range(2)]
        x_scale = [keep.tile([P, HALF], U8, name=f"x_scale{h}", align_bytes=64) for h in range(2)]
        dense_third = keep.tile([P, 3, QUARTER], BF16, name="dense_third", align_bytes=64)
        dense_fourth = [keep.tile([P, 2, QUARTER], BF16, name=f"dense_fourth{w}", align_bytes=64) for w in range(2)]

        def into_place(l, points):
            nc.vector.tensor_copy(out=grouped[:, points, l], in_=looked_up(l, points.start, points.stop - points.start))

        def dense(l, points, row):
            nc.scalar.activation(row, looked_up(l, points.start, QUARTER), COPY)

        def by_point(rows):
            return rows[:].rearrange("p l v -> p v l")

        for l in (0, 1):
            into_place(l, slice(0, HALF))
            dense(l, fourth, dense_fourth[0][:, l, :])
            dense(l, third, dense_third[:, l, :])
        nc.vector.tensor_copy(out=grouped[:, fourth, 0:2], in_=by_point(dense_fourth[0]))
        into_place(2, slice(0, HALF))
        dense(2, third, dense_third[:, 2, :])
        dense(2, fourth, dense_fourth[1][:, 0, :])
        nc.vector.tensor_copy(out=grouped[:, third, 0:3], in_=by_point(dense_third))
        into_place(3, slice(0, HALF))
        into_place(3, third)
        dense(3, fourth, dense_fourth[1][:, 1, :])
        nc.scalar.copy(out=grouped[:, fourth, 2:4], in_=by_point(dense_fourth[1]))
        for points in (slice(0, HALF), third, fourth):
            h, cols = points.start // HALF, slice(points.start % HALF, (points.stop - 1) % HALF + 1)
            nc.vector.quantize_mx(
                out=x_code[h][:, cols].bitcast(FP8X4),
                scales=x_scale[h][:, cols],
                in_=grouped[:, points, :].rearrange("p v l -> p (v l)"),
            )

        halves = [slice(h * HALF, (h + 1) * HALF) for h in range(2)]
        result = keep.tile([P, D, V], F32, name="result", align_bytes=256)

        def product(j, h):
            cols = slice(j * P, (j + 1) * P)
            acc = psum.tile([P, HALF], F32, name=f"acc{j}_{h}")
            nc.tensor.matmul_mx(
                out=acc[:],
                lhsT=w_code[:, cols].bitcast(FP8X4),
                lhsT_scale=w_scale[4 * j :, :],
                rhs=x_code[h][:].bitcast(FP8X4),
                rhs_scale=x_scale[h][:],
                start=True,
                stop=True,
            )
            nc.vector.tensor_copy(out=result[:, j, halves[h]], in_=acc[:])

        out_blocks = out.rearrange("(j p) v -> p j v", p=P)

        def store(blocks, h, queue):
            queue.dma_start(out=out_blocks[:, blocks, halves[h]], in_=result[:, blocks, halves[h]])

        product(0, 0)
        store(slice(0, 1), 0, nc.sync)
        product(1, 0)
        store(slice(1, 2), 0, nc.scalar)
        product(2, 0)
        product(3, 0)
        store(slice(2, 4), 0, nc.sync)
        for pair, queue in ((0, nc.scalar), (2, nc.sync)):
            product(pair, 1)
            product(pair + 1, 1)
            store(slice(pair, pair + 2), 1, queue)
